import numpy as np
import ml_dtypes


def mxq(x, axis, fmt="e4m3"):
    dtype, down = {"e4m3": (ml_dtypes.float8_e4m3fn, 7), "e5m2": (ml_dtypes.float8_e5m2, 14)}[fmt]
    v = np.moveaxis(np.asarray(x, np.float32).astype(ml_dtypes.bfloat16).astype(np.float64), axis, -1)
    blocks = v.reshape(v.shape[:-1] + (-1, 32))
    amax = np.abs(blocks).max(-1, keepdims=True)
    byte = np.maximum(np.where(amax > 0, np.frexp(amax)[1] - 1 + 127, 0) - down, 1)
    scale = np.exp2(byte - 127.0)
    codes = (blocks / scale).astype(np.float32).astype(dtype).astype(np.float64)
    return np.moveaxis((codes * scale).reshape(v.shape), -1, axis)


WIDE = False


def mx_kscale(k):
    if not WIDE:
        return np.ones(k)
    levels = np.array([10, -10, 5, -5, 0])
    if k % 512:
        return np.exp2(np.random.permutation(np.resize(levels, k // 32))).repeat(32)
    a = np.empty((k // 512, 16))
    for p in range(k // 512):
        a[p, :8] = np.random.permutation(np.resize(levels, 8))
        for g in range(8):
            far = levels[np.abs(levels - a[p, g]) >= 10]
            a[p, g + 8] = far[np.random.randint(len(far))]
    return np.exp2(a.ravel()).repeat(32)


def f64(x):
    return np.asarray(x).astype(np.float64)


def striped8(idx):
    return np.concatenate([v.reshape(-1, 16).T for v in idx]).astype(np.uint16)


def unstriped8(offs):
    return np.stack([offs[16 * g:16 * g + 16].T.reshape(-1) for g in range(8)]).astype(np.int64)


def gelu(v):
    return 0.5 * v * (1.0 + np.tanh(np.sqrt(2.0 / np.pi) * (v + 0.044715 * v**3)))


K, M, T, S = 1536, 512, 1024, 512


def setup_inputs():
    n = np.random.standard_normal
    s = mx_kscale(K)[:, None]
    return {
        "xT": (n((K, T)) * s).astype(np.float32),
        "w": (n((K, M)) / np.sqrt(K) / s).astype(np.float32),
        "wgt": np.repeat(np.random.uniform(0.5, 2.0, (8, S)), 16, axis=0).astype(np.float32),
        "b": (0.3 * n(512)).astype(np.float32),
        "wgo": np.repeat(np.random.uniform(0.5, 2.0, (8, S)), 16, axis=0).astype(np.float32),
        "offs": striped8(np.stack([np.random.permutation(T)[:S] for _ in range(8)])),
        "offs2": striped8(np.stack([np.random.permutation(T)[:S] for _ in range(8)])),
    }


def reference(xT, w, wgt, b, wgo, offs, offs2):
    idx = unstriped8(offs)
    group = np.arange(K) % 512 // 64
    xg = f64(wgt)[np.arange(K) // 4 % 128] * f64(xT)[np.arange(K)[:, None], idx[group]]
    xT_ = mxq(xg, 0, "e4m3")
    w_ = mxq(f64(w), 0, "e4m3")
    y = w_.T @ xT_
    place = unstriped8(offs2)[np.arange(M) % 128 // 16]
    out = np.zeros((M, T))
    out[np.arange(M)[:, None], place] = f64(wgo)[np.arange(M) % 128] * (gelu(y + f64(b)[:, None]))
    return out

@@ -1,0 +1,185 @@
+from contextlib import ExitStack
+
+import concourse.mybir as mybir
+
+K, M, T, S = 1536, 512, 1024, 512
+FLOPS = 2 * K * M * S
+
+F32 = mybir.dt.float32
+BF16 = mybir.dt.bfloat16
+U32 = mybir.dt.uint32
+U16 = mybir.dt.uint16
+U8 = mybir.dt.uint8
+FP8X4 = mybir.dt.float8_e4m3fn_x4
+MULT = mybir.AluOpType.mult
+GELU = mybir.ActivationFunctionType.Gelu_apprx_tanh
+
+P = 128
+PACK = 4
+K_PASS = P * PACK
+PASSES = K // K_PASS
+HALVES = 2
+J = S // HALVES
+M_TILES = M // P
+LIST = S // 16
+LIST_HALF = LIST // HALVES
+
+
+def tile_list_hboth_gelu_kernel(tc, xT, w, wgt, b, wgo, offs, offs2, out):
+    nc = tc.nc
+    with ExitStack() as ctx:
+        keep = ctx.enter_context(tc.tile_pool(name="keep", bufs=1))
+        psum = ctx.enter_context(tc.psum_pool(name="psum", bufs=1))
+
+        lists_in = keep.tile([P, LIST], U16, name="lists_in")
+        lists_out = keep.tile([P, LIST], U16, name="lists_out")
+        bias = keep.tile([P, M_TILES], F32, name="bias")
+        scratch = keep.tile([P, 2], F32, name="scratch")
+        wgt_t = [keep.tile([P, J], F32, name=f"wgt{h}") for h in range(HALVES)]
+        wgo_t = keep.tile([P, S], F32, name="wgo_t")
+        x = [[keep.tile([P, T], F32, name=f"x{a}_{i}") for i in range(PACK)] for a in range(PASSES)]
+        window = [keep.tile([P, T], F32, name=f"window{m}") for m in range(M_TILES)]
+        picked = [keep.tile([P, PACK, S], F32, name=f"picked{a}") for a in range(PASSES)]
+        x_codes = [keep.tile([P, S], U32, name=f"xc{a}", align_bytes=64) for a in range(PASSES)]
+        x_scales = [keep.tile([P, S], U8, name=f"xs{a}", align_bytes=64) for a in range(PASSES)]
+        w_bf = [keep.tile([P, PASSES * P, PACK], BF16, name=f"wbf{m}", align_bytes=64) for m in range(M_TILES)]
+        w_codes = [keep.tile([P, PASSES * P], U32, name=f"wc{m}", align_bytes=64) for m in range(M_TILES)]
+        w_scales = [keep.tile([P, PASSES * P], U8, name=f"ws{m}", align_bytes=64) for m in range(M_TILES)]
+        y = [[keep.tile([P, J], F32, name=f"y{m}_{h}") for h in range(HALVES)] for m in range(M_TILES)]
+        acc = [[psum.tile([P, J], F32, name=f"acc{m}_{h}") for h in range(HALVES)] for m in range(M_TILES)]
+
+        def load_x(a, i):
+            planes = xT[a * K_PASS : (a + 1) * K_PASS, :].rearrange("(p i) t -> p i t", i=PACK)
+            nc.sync.dma_start(out=x[a][i][:], in_=planes[:, i, :])
+
+        nc.gpsimd.memset(scratch[:], 0.0)
+        nc.scalar.dma_start(out=wgt_t[0][:], in_=wgt[:, 0:J])
+        nc.scalar.activation(scratch[:, 1:2], scratch[:, 0:1], GELU)
+
+        nc.sync.dma_start(lists_in[:], offs)
+        load_x(0, 0)
+        nc.sync.dma_start(out=wgt_t[1][:], in_=wgt[:, J:S])
+        for i in range(1, PACK):
+            load_x(0, i)
+        nc.sync.dma_start(lists_out[:], offs2)
+        with nc.allow_non_contiguous_dma(reason="one bias value to a partition"):
+            nc.sync.dma_start(out=bias[:], in_=b.rearrange("(m p) -> p m", p=P))
+        for i in range(PACK):
+            load_x(1, i)
+        for i in range(PACK):
+            load_x(2, i)
+        nc.sync.dma_start(out=wgo_t[:], in_=wgo)
+
+        nc.vector.memset(window[0][:], 0.0)
+        nc.vector.memset(window[1][:], 0.0)
+        nc.gpsimd.memset(window[2][:], 0.0)
+        nc.gpsimd.memset(window[3][:], 0.0)
+
+        def gather(a, h, i):
+            nc.vector.tensor_tensor(
+                picked[a][:, i, h * J : (h + 1) * J],
+                x[a][i][:].indirect(lists_in[:, h * LIST_HALF : (h + 1) * LIST_HALF]),
+                wgt_t[h][:],
+                MULT,
+            )
+
+        def round_x(x_bf, a, j0, j1):
+            nc.scalar.copy(out=x_bf[:], in_=picked[a][:, :, j0:j1].rearrange("p i j -> p j i"))
+
+        def quantize_x(x_bf, a, j0, j1):
+            nc.vector.quantize_mx(
+                out=x_codes[a][:, j0:j1].bitcast(FP8X4),
+                scales=x_scales[a][:, j0:j1],
+                in_=x_bf[:].rearrange("p j i -> p (j i)"),
+            )
+
+        def load_w(m, slot):
+            raw = keep.tile([P, PASSES, PACK, P], F32, name=f"wraw{m}", tag=slot, align_bytes=64)
+            for a in range(PASSES):
+                rows = w[a * K_PASS : (a + 1) * K_PASS, m * P : (m + 1) * P]
+                nc.sync.dma_start(out=raw[:, a], in_=rows.rearrange("(p i) n -> p i n", i=PACK))
+            return raw
+
+        def quantize_w(m, raw):
+            for a in range(PASSES):
+                nc.scalar.copy(out=w_bf[m][:, a * P : (a + 1) * P, :], in_=raw[:, a].rearrange("p i n -> p n i"))
+            for a0, a1 in ((0, 2), (2, 3)):
+                cols = slice(a0 * P, a1 * P)
+                nc.vector.quantize_mx(
+                    out=w_codes[m][:, cols].bitcast(FP8X4),
+                    scales=w_scales[m][:, cols],
+                    in_=w_bf[m][:, cols, :].rearrange("p n i -> p (n i)"),
+                )
+
+        def project(m, h):
+            js = slice(h * J, (h + 1) * J)
+            for a in range(PASSES):
+                cols = slice(a * P, (a + 1) * P)
+                nc.tensor.matmul_mx(
+                    out=acc[m][h][:],
+                    lhsT=w_codes[m][:, cols].bitcast(FP8X4),
+                    lhsT_scale=w_scales[m][:, cols],
+                    rhs=x_codes[a][:, js].bitcast(FP8X4),
+                    rhs_scale=x_scales[a][:, js],
+                    start=(a == 0),
+                    stop=(a == PASSES - 1),
+                )
+            nc.scalar.activation(y[m][h][:], acc[m][h][:], GELU, bias=bias[:, m : m + 1])
+
+        def scatter(m, h):
+            nc.vector.tensor_tensor(
+                window[m][:].indirect(lists_out[:, h * LIST_HALF : (h + 1) * LIST_HALF]),
+                y[m][h][:],
+                wgo_t[:, h * J : (h + 1) * J],
+                MULT,
+            )
+
+        def store(m):
+            nc.sync.dma_start(out=out[m * P : (m + 1) * P, :], in_=window[m][:])
+
+        raw = []
+        for a in range(PASSES - 1):
+            for i in range(PACK):
+                gather(a, 0, i)
+                gather(a, 1, i)
+            x_bf = keep.tile([P, S, PACK], BF16, name=f"xbf{a}", align_bytes=64)
+            for h in range(HALVES):
+                nc.scalar.copy(
+                    out=x_bf[:, h * J : (h + 1) * J, :],
+                    in_=picked[a][:, :, h * J : (h + 1) * J].rearrange("p i j -> p j i"),
+                )
+            quantize_x(x_bf, a, 0, S)
+            raw.append(load_w(a, f"xbf{a}"))
+        last = PASSES - 1
+        for h in range(HALVES):
+            for i in range(PACK):
+                gather(last, h, i)
+            x_bf = keep.tile([P, J, PACK], BF16, name=f"xbf{last}_{h}", align_bytes=64)
+            round_x(x_bf, last, h * J, (h + 1) * J)
+            quantize_x(x_bf, last, h * J, (h + 1) * J)
+            raw.append(load_w(last + h, f"xbf{last}_{h}"))
+
+        quantize_w(0, raw[0])
+        project(0, 0)
+        project(0, 1)
+        scatter(0, 0)
+        quantize_w(1, raw[1])
+        project(1, 0)
+        project(1, 1)
+        scatter(0, 1)
+        store(0)
+        scatter(1, 0)
+        quantize_w(2, raw[2])
+        project(2, 0)
+        project(2, 1)
+        scatter(1, 1)
+        store(1)
+        quantize_w(3, raw[3])
+        project(3, 0)
+        project(3, 1)
+        scatter(2, 0)
+        scatter(3, 0)
+        scatter(2, 1)
+        store(2)
+        scatter(3, 1)
+        store(3)

@@ -1,6 +1,7 @@
 from contextlib import ExitStack
 
 import concourse.mybir as mybir
+from concourse.masks import make_identity
 
 K, M, T, S = 1536, 512, 1024, 512
 FLOPS = 2 * K * M * S
@@ -20,6 +21,7 @@ K_PASS = P * PACK
 PASSES = K // K_PASS
 HALVES = 2
 J = S // HALVES
+W_COLS = M // HALVES
 M_TILES = M // P
 LIST = S // 16
 LIST_HALF = LIST // HALVES
@@ -33,103 +35,126 @@ def tile_list_hboth_gelu_kernel(tc, xT, w, wgt, b, wgo, offs, offs2, out):
 
         lists_in = keep.tile([P, LIST], U16, name="lists_in")
         lists_out = keep.tile([P, LIST], U16, name="lists_out")
+        bias_rows = keep.tile([P, P], F32, name="bias_rows")
+        ident = keep.tile([P, P], F32, name="ident")
         bias = keep.tile([P, M_TILES], F32, name="bias")
         scratch = keep.tile([P, 2], F32, name="scratch")
         wgt_t = [keep.tile([P, J], F32, name=f"wgt{h}") for h in range(HALVES)]
+        wgt_late = keep.tile([P, J], F32, name="wgt_late")
         wgo_t = keep.tile([P, S], F32, name="wgo_t")
         x = [[keep.tile([P, T], F32, name=f"x{a}_{i}") for i in range(PACK)] for a in range(PASSES)]
+        w_raw = [[keep.tile([P, PACK, W_COLS], F32, name=f"wraw{a}_{c}") for c in range(HALVES)] for a in range(PASSES)]
         window = [keep.tile([P, T], F32, name=f"window{m}") for m in range(M_TILES)]
-        picked = [keep.tile([P, PACK, S], F32, name=f"picked{a}") for a in range(PASSES)]
+        picked = [[keep.tile([P, PACK, J], F32, name=f"picked{a}_{h}") for h in range(HALVES)] for a in range(PASSES)]
+        x_bf = [[keep.tile([P, J, PACK], BF16, name=f"xbf{a}_{h}", align_bytes=64) for h in range(HALVES)] for a in range(PASSES)]
+        w_bf = [[keep.tile([P, W_COLS, PACK], BF16, name=f"wbf{a}_{c}", align_bytes=64) for c in range(HALVES)] for a in range(PASSES)]
         x_codes = [keep.tile([P, S], U32, name=f"xc{a}", align_bytes=64) for a in range(PASSES)]
         x_scales = [keep.tile([P, S], U8, name=f"xs{a}", align_bytes=64) for a in range(PASSES)]
-        w_bf = [keep.tile([P, PASSES * P, PACK], BF16, name=f"wbf{m}", align_bytes=64) for m in range(M_TILES)]
-        w_codes = [keep.tile([P, PASSES * P], U32, name=f"wc{m}", align_bytes=64) for m in range(M_TILES)]
-        w_scales = [keep.tile([P, PASSES * P], U8, name=f"ws{m}", align_bytes=64) for m in range(M_TILES)]
-        y = [[keep.tile([P, J], F32, name=f"y{m}_{h}") for h in range(HALVES)] for m in range(M_TILES)]
-        acc = [[psum.tile([P, J], F32, name=f"acc{m}_{h}") for h in range(HALVES)] for m in range(M_TILES)]
+        w_codes = [[keep.tile([P, W_COLS], U32, name=f"wc{a}_{c}", align_bytes=64) for c in range(HALVES)] for a in range(PASSES)]
+        w_scales = [[keep.tile([P, W_COLS], U8, name=f"ws{a}_{c}", align_bytes=64) for c in range(HALVES)] for a in range(PASSES)]
+        y = [keep.tile([P, S], F32, name=f"y{m}") for m in range(M_TILES)]
+        bias_bank = psum.tile([P, P], F32, name="bias_bank", tag="acc3_1")
+        acc_half = [[psum.tile([P, J], F32, name=f"acc{m}_{h}", tag=f"acc{m}_{h}") for h in range(HALVES)] for m in range(M_TILES)]
 
         def load_x(a, i):
             planes = xT[a * K_PASS : (a + 1) * K_PASS, :].rearrange("(p i) t -> p i t", i=PACK)
             nc.sync.dma_start(out=x[a][i][:], in_=planes[:, i, :])
 
+        def load_w(a, c):
+            rows = w[a * K_PASS : (a + 1) * K_PASS, c * W_COLS : (c + 1) * W_COLS]
+            nc.sync.dma_start(out=w_raw[a][c][:], in_=rows.rearrange("(p i) n -> p i n", i=PACK))
+
         nc.gpsimd.memset(scratch[:], 0.0)
-        nc.scalar.dma_start(out=wgt_t[0][:], in_=wgt[:, 0:J])
+        nc.gpsimd.memset(bias_rows[:], 0.0)
         nc.scalar.activation(scratch[:, 1:2], scratch[:, 0:1], GELU)
 
         nc.sync.dma_start(lists_in[:], offs)
+        nc.scalar.dma_start(out=wgt_t[0][:], in_=wgt[:, 0:J])
         load_x(0, 0)
         nc.sync.dma_start(out=wgt_t[1][:], in_=wgt[:, J:S])
-        for i in range(1, PACK):
-            load_x(0, i)
+        load_x(0, 1)
+        load_x(0, 2)
+        load_x(0, 3)
+        load_w(0, 0)
+        load_x(1, 0)
+        load_x(1, 1)
+        load_x(1, 2)
+        load_w(1, 0)
+        load_x(1, 3)
+        load_x(2, 0)
+        load_x(2, 1)
+        load_w(2, 0)
+        load_x(2, 2)
+        load_x(2, 3)
+        nc.sync.dma_start(out=wgt_late[:], in_=wgt[:, J:S])
         nc.sync.dma_start(lists_out[:], offs2)
-        with nc.allow_non_contiguous_dma(reason="one bias value to a partition"):
-            nc.sync.dma_start(out=bias[:], in_=b.rearrange("(m p) -> p m", p=P))
-        for i in range(PACK):
-            load_x(1, i)
-        for i in range(PACK):
-            load_x(2, i)
+        nc.sync.dma_start(out=bias_rows[0:M_TILES, :], in_=b.rearrange("(m p) -> m p", p=P))
         nc.sync.dma_start(out=wgo_t[:], in_=wgo)
+        load_w(0, 1)
+        load_w(1, 1)
+        load_w(2, 1)
 
         nc.vector.memset(window[0][:], 0.0)
         nc.vector.memset(window[1][:], 0.0)
+        make_identity(nc, ident[:])
         nc.gpsimd.memset(window[2][:], 0.0)
         nc.gpsimd.memset(window[3][:], 0.0)
+        nc.tensor.transpose(bias_bank[:], bias_rows[:], ident[:])
+        nc.scalar.copy(out=bias[:], in_=bias_bank[:, 0:M_TILES])
 
         def gather(a, h, i):
             nc.vector.tensor_tensor(
-                picked[a][:, i, h * J : (h + 1) * J],
+                picked[a][h][:, i, :],
                 x[a][i][:].indirect(lists_in[:, h * LIST_HALF : (h + 1) * LIST_HALF]),
-                wgt_t[h][:],
+                (wgt_late if (a, h) == (2, 1) and i >= 2 else wgt_t[h])[:],
                 MULT,
             )
 
-        def round_x(x_bf, a, j0, j1):
-            nc.scalar.copy(out=x_bf[:], in_=picked[a][:, :, j0:j1].rearrange("p i j -> p j i"))
-
-        def quantize_x(x_bf, a, j0, j1):
-            nc.vector.quantize_mx(
-                out=x_codes[a][:, j0:j1].bitcast(FP8X4),
-                scales=x_scales[a][:, j0:j1],
-                in_=x_bf[:].rearrange("p j i -> p (j i)"),
+        def interleave(copy, grouped, planes):
+            copy(
+                out=grouped.rearrange("p (c q) i -> p c i q", q=4),
+                in_=planes.rearrange("p i (c q) -> p c i q", q=4),
             )
 
-        def load_w(m, slot):
-            raw = keep.tile([P, PASSES, PACK, P], F32, name=f"wraw{m}", tag=slot, align_bytes=64)
-            for a in range(PASSES):
-                rows = w[a * K_PASS : (a + 1) * K_PASS, m * P : (m + 1) * P]
-                nc.sync.dma_start(out=raw[:, a], in_=rows.rearrange("(p i) n -> p i n", i=PACK))
-            return raw
+        def round_x(a, h):
+            interleave(nc.scalar.copy, x_bf[a][h][:], picked[a][h][:])
 
-        def quantize_w(m, raw):
-            for a in range(PASSES):
-                nc.scalar.copy(out=w_bf[m][:, a * P : (a + 1) * P, :], in_=raw[:, a].rearrange("p i n -> p n i"))
-            for a0, a1 in ((0, 2), (2, 3)):
-                cols = slice(a0 * P, a1 * P)
-                nc.vector.quantize_mx(
-                    out=w_codes[m][:, cols].bitcast(FP8X4),
-                    scales=w_scales[m][:, cols],
-                    in_=w_bf[m][:, cols, :].rearrange("p n i -> p (n i)"),
-                )
-
-        def project(m, h):
+        def quantize_x(a, h):
             js = slice(h * J, (h + 1) * J)
+            nc.vector.quantize_mx(
+                out=x_codes[a][:, js].bitcast(FP8X4),
+                scales=x_scales[a][:, js],
+                in_=x_bf[a][h][:].rearrange("p j i -> p (j i)"),
+            )
+
+        def round_w(copy, a, c, n0, n1):
+            interleave(copy, w_bf[a][c][:, n0:n1, :], w_raw[a][c][:, :, n0:n1])
+
+        def quantize_w(a, c):
+            nc.vector.quantize_mx(
+                out=w_codes[a][c][:].bitcast(FP8X4),
+                scales=w_scales[a][c][:],
+                in_=w_bf[a][c][:].rearrange("p n i -> p (n i)"),
+            )
+
+        def multiply(bank, m, j0, j1):
+            c, n0 = m // 2, m % 2 * P
             for a in range(PASSES):
-                cols = slice(a * P, (a + 1) * P)
                 nc.tensor.matmul_mx(
-                    out=acc[m][h][:],
-                    lhsT=w_codes[m][:, cols].bitcast(FP8X4),
-                    lhsT_scale=w_scales[m][:, cols],
-                    rhs=x_codes[a][:, js].bitcast(FP8X4),
-                    rhs_scale=x_scales[a][:, js],
+                    out=bank[:],
+                    lhsT=w_codes[a][c][:, n0 : n0 + P].bitcast(FP8X4),
+                    lhsT_scale=w_scales[a][c][:, n0 : n0 + P],
+                    rhs=x_codes[a][:, j0:j1].bitcast(FP8X4),
+                    rhs_scale=x_scales[a][:, j0:j1],
                     start=(a == 0),
                     stop=(a == PASSES - 1),
                 )
-            nc.scalar.activation(y[m][h][:], acc[m][h][:], GELU, bias=bias[:, m : m + 1])
+            nc.scalar.activation(y[m][:, j0:j1], bank[:], GELU, bias=bias[:, m : m + 1])
 
         def scatter(m, h):
             nc.vector.tensor_tensor(
                 window[m][:].indirect(lists_out[:, h * LIST_HALF : (h + 1) * LIST_HALF]),
-                y[m][h][:],
+                y[m][:, h * J : (h + 1) * J],
                 wgo_t[:, h * J : (h + 1) * J],
                 MULT,
             )
@@ -137,48 +162,73 @@ def tile_list_hboth_gelu_kernel(tc, xT, w, wgt, b, wgo, offs, offs2, out):
         def store(m):
             nc.sync.dma_start(out=out[m * P : (m + 1) * P, :], in_=window[m][:])
 
-        raw = []
-        for a in range(PASSES - 1):
-            for i in range(PACK):
-                gather(a, 0, i)
-                gather(a, 1, i)
-            x_bf = keep.tile([P, S, PACK], BF16, name=f"xbf{a}", align_bytes=64)
-            for h in range(HALVES):
-                nc.scalar.copy(
-                    out=x_bf[:, h * J : (h + 1) * J, :],
-                    in_=picked[a][:, :, h * J : (h + 1) * J].rearrange("p i j -> p j i"),
-                )
-            quantize_x(x_bf, a, 0, S)
-            raw.append(load_w(a, f"xbf{a}"))
-        last = PASSES - 1
-        for h in range(HALVES):
-            for i in range(PACK):
-                gather(last, h, i)
-            x_bf = keep.tile([P, J, PACK], BF16, name=f"xbf{last}_{h}", align_bytes=64)
-            round_x(x_bf, last, h * J, (h + 1) * J)
-            quantize_x(x_bf, last, h * J, (h + 1) * J)
-            raw.append(load_w(last + h, f"xbf{last}_{h}"))
-
-        quantize_w(0, raw[0])
-        project(0, 0)
-        project(0, 1)
+        gather(0, 0, 0)
+        gather(0, 1, 0)
+        gather(0, 0, 1)
+        gather(0, 1, 1)
+        gather(0, 0, 2)
+        gather(0, 1, 2)
+        gather(0, 0, 3)
+        round_x(0, 0)
+        quantize_x(0, 0)
+        gather(0, 1, 3)
+        round_x(0, 1)
+        quantize_x(0, 1)
+        gather(1, 0, 0)
+        gather(1, 1, 0)
+        gather(1, 0, 1)
+        gather(1, 1, 1)
+        gather(1, 0, 2)
+        gather(1, 0, 3)
+        round_x(1, 0)
+        quantize_x(1, 0)
+        gather(1, 1, 2)
+        gather(1, 1, 3)
+        round_x(1, 1)
+        quantize_x(1, 1)
+        round_w(nc.vector.tensor_copy, 0, 0, 0, W_COLS)
+        quantize_w(0, 0)
+        gather(2, 0, 0)
+        gather(2, 1, 0)
+        gather(2, 0, 1)
+        round_w(nc.scalar.copy, 1, 0, 0, P)
+        round_w(nc.scalar.copy, 1, 0, P, W_COLS)
+        quantize_w(1, 0)
+        gather(2, 0, 2)
+        gather(2, 0, 3)
+        round_x(2, 0)
+        quantize_x(2, 0)
+        gather(2, 1, 1)
+        gather(2, 1, 2)
+        round_w(nc.scalar.copy, 2, 0, 0, P)
+        round_w(nc.scalar.copy, 2, 0, P, W_COLS)
+        quantize_w(2, 0)
+        gather(2, 1, 3)
+        round_x(2, 1)
+        quantize_x(2, 1)
+        multiply(acc_half[0][0], 0, 0, J)
+        round_w(nc.vector.tensor_copy, 0, 1, 0, W_COLS)
+        quantize_w(0, 1)
+        multiply(acc_half[1][0], 1, 0, J)
+        round_w(nc.scalar.copy, 1, 1, 0, P)
+        round_w(nc.scalar.copy, 1, 1, P, W_COLS)
+        quantize_w(1, 1)
         scatter(0, 0)
-        quantize_w(1, raw[1])
-        project(1, 0)
-        project(1, 1)
+        scatter(1, 0)
+        multiply(acc_half[0][1], 0, J, S)
+        round_w(nc.scalar.copy, 2, 1, 0, W_COLS)
+        quantize_w(2, 1)
+        multiply(acc_half[1][1], 1, J, S)
         scatter(0, 1)
         store(0)
-        scatter(1, 0)
-        quantize_w(2, raw[2])
-        project(2, 0)
-        project(2, 1)
         scatter(1, 1)
         store(1)
-        quantize_w(3, raw[3])
-        project(3, 0)
-        project(3, 1)
+        multiply(acc_half[2][0], 2, 0, J)
+        multiply(acc_half[3][0], 3, 0, J)
         scatter(2, 0)
         scatter(3, 0)
+        multiply(acc_half[2][1], 2, J, S)
+        multiply(acc_half[3][1], 3, J, S)
         scatter(2, 1)
         store(2)
         scatter(3, 1)

@@ -39,16 +39,16 @@ def tile_list_hboth_gelu_kernel(tc, xT, w, wgt, b, wgo, offs, offs2, out):
         ident = keep.tile([P, P], F32, name="ident")
         bias = keep.tile([P, M_TILES], F32, name="bias")
         scratch = keep.tile([P, 2], F32, name="scratch")
-        wgt_t = [keep.tile([P, J], F32, name=f"wgt{h}") for h in range(HALVES)]
+        wgt_t = [keep.tile([P, J], F32, name=f"wgt{h}", align_bytes=64) for h in range(HALVES)]
         wgt_late = keep.tile([P, J], F32, name="wgt_late")
         wgo_t = keep.tile([P, S], F32, name="wgo_t")
         x = [[keep.tile([P, T], F32, name=f"x{a}_{i}") for i in range(PACK)] for a in range(PASSES)]
         w_raw = [[keep.tile([P, PACK, W_COLS], F32, name=f"wraw{a}_{c}") for c in range(HALVES)] for a in range(PASSES)]
         window = [keep.tile([P, T], F32, name=f"window{m}") for m in range(M_TILES)]
         picked = [[keep.tile([P, PACK, J], F32, name=f"picked{a}_{h}") for h in range(HALVES)] for a in range(PASSES)]
-        x_bf = [[keep.tile([P, J, PACK], BF16, name=f"xbf{a}_{h}", align_bytes=64) for h in range(HALVES)] for a in range(PASSES)]
+        x_bf = [keep.tile([P, S, PACK], BF16, name=f"xbf{a}", align_bytes=64) for a in range(PASSES)]
         w_bf = [[keep.tile([P, W_COLS, PACK], BF16, name=f"wbf{a}_{c}", align_bytes=64) for c in range(HALVES)] for a in range(PASSES)]
-        x_codes = [keep.tile([P, S], U32, name=f"xc{a}", align_bytes=64) for a in range(PASSES)]
+        x_codes = [keep.tile([P, S], U32, name=f"xc{a}", tag=("xc0", "wgt0", "xc2")[a], align_bytes=64) for a in range(PASSES)]
         x_scales = [keep.tile([P, S], U8, name=f"xs{a}", align_bytes=64) for a in range(PASSES)]
         w_codes = [[keep.tile([P, W_COLS], U32, name=f"wc{a}_{c}", align_bytes=64) for c in range(HALVES)] for a in range(PASSES)]
         w_scales = [[keep.tile([P, W_COLS], U8, name=f"ws{a}_{c}", align_bytes=64) for c in range(HALVES)] for a in range(PASSES)]
@@ -75,18 +75,18 @@ def tile_list_hboth_gelu_kernel(tc, xT, w, wgt, b, wgo, offs, offs2, out):
         load_x(0, 1)
         load_x(0, 2)
         load_x(0, 3)
-        load_w(0, 0)
         load_x(1, 0)
         load_x(1, 1)
         load_x(1, 2)
-        load_w(1, 0)
+        load_w(0, 0)
         load_x(1, 3)
         load_x(2, 0)
         load_x(2, 1)
-        load_w(2, 0)
         load_x(2, 2)
         load_x(2, 3)
         nc.sync.dma_start(out=wgt_late[:], in_=wgt[:, J:S])
+        load_w(1, 0)
+        load_w(2, 0)
         nc.sync.dma_start(lists_out[:], offs2)
         nc.sync.dma_start(out=bias_rows[0:M_TILES, :], in_=b.rearrange("(m p) -> m p", p=P))
         nc.sync.dma_start(out=wgo_t[:], in_=wgo)
@@ -106,7 +106,7 @@ def tile_list_hboth_gelu_kernel(tc, xT, w, wgt, b, wgo, offs, offs2, out):
             nc.vector.tensor_tensor(
                 picked[a][h][:, i, :],
                 x[a][i][:].indirect(lists_in[:, h * LIST_HALF : (h + 1) * LIST_HALF]),
-                (wgt_late if (a, h) == (2, 1) and i >= 2 else wgt_t[h])[:],
+                (wgt_late if (a, h) == (2, 1) and i >= 1 else wgt_t[h])[:],
                 MULT,
             )
 
@@ -117,14 +117,21 @@ def tile_list_hboth_gelu_kernel(tc, xT, w, wgt, b, wgo, offs, offs2, out):
             )
 
         def round_x(a, h):
-            interleave(nc.scalar.copy, x_bf[a][h][:], picked[a][h][:])
+            interleave(nc.scalar.copy, x_bf[a][:, h * J : (h + 1) * J, :], picked[a][h][:])
 
         def quantize_x(a, h):
             js = slice(h * J, (h + 1) * J)
             nc.vector.quantize_mx(
                 out=x_codes[a][:, js].bitcast(FP8X4),
                 scales=x_scales[a][:, js],
-                in_=x_bf[a][h][:].rearrange("p j i -> p (j i)"),
+                in_=x_bf[a][:, js, :].rearrange("p j i -> p (j i)"),
+            )
+
+        def quantize_x_pass(a):
+            nc.vector.quantize_mx(
+                out=x_codes[a][:].bitcast(FP8X4),
+                scales=x_scales[a][:],
+                in_=x_bf[a][:].rearrange("p j i -> p (j i)"),
             )
 
         def round_w(copy, a, c, n0, n1):
@@ -179,45 +186,44 @@ def tile_list_hboth_gelu_kernel(tc, xT, w, wgt, b, wgo, offs, offs2, out):
         gather(1, 0, 1)
         gather(1, 1, 1)
         gather(1, 0, 2)
+        gather(1, 1, 2)
         gather(1, 0, 3)
         round_x(1, 0)
-        quantize_x(1, 0)
-        gather(1, 1, 2)
         gather(1, 1, 3)
         round_x(1, 1)
-        quantize_x(1, 1)
-        round_w(nc.vector.tensor_copy, 0, 0, 0, W_COLS)
+        quantize_x_pass(1)
+        round_w(nc.scalar.copy, 0, 0, 0, P)
+        round_w(nc.scalar.copy, 0, 0, P, W_COLS)
         quantize_w(0, 0)
         gather(2, 0, 0)
         gather(2, 1, 0)
-        gather(2, 0, 1)
         round_w(nc.scalar.copy, 1, 0, 0, P)
         round_w(nc.scalar.copy, 1, 0, P, W_COLS)
         quantize_w(1, 0)
+        gather(2, 0, 1)
+        gather(2, 1, 1)
         gather(2, 0, 2)
         gather(2, 0, 3)
         round_x(2, 0)
         quantize_x(2, 0)
-        gather(2, 1, 1)
         gather(2, 1, 2)
-        round_w(nc.scalar.copy, 2, 0, 0, P)
-        round_w(nc.scalar.copy, 2, 0, P, W_COLS)
-        quantize_w(2, 0)
         gather(2, 1, 3)
         round_x(2, 1)
         quantize_x(2, 1)
+        round_w(nc.vector.tensor_copy, 2, 0, 0, W_COLS)
+        quantize_w(2, 0)
         multiply(acc_half[0][0], 0, 0, J)
-        round_w(nc.vector.tensor_copy, 0, 1, 0, W_COLS)
-        quantize_w(0, 1)
         multiply(acc_half[1][0], 1, 0, J)
-        round_w(nc.scalar.copy, 1, 1, 0, P)
-        round_w(nc.scalar.copy, 1, 1, P, W_COLS)
-        quantize_w(1, 1)
+        round_w(nc.scalar.copy, 0, 1, 0, P)
+        round_w(nc.scalar.copy, 0, 1, P, W_COLS)
+        quantize_w(0, 1)
         scatter(0, 0)
+        round_w(nc.scalar.copy, 1, 1, 0, W_COLS)
+        quantize_w(1, 1)
         scatter(1, 0)
-        multiply(acc_half[0][1], 0, J, S)
         round_w(nc.scalar.copy, 2, 1, 0, W_COLS)
         quantize_w(2, 1)
+        multiply(acc_half[0][1], 0, J, S)
         multiply(acc_half[1][1], 1, J, S)
         scatter(0, 1)
         store(0)

@@ -41,14 +41,14 @@ def tile_list_hboth_gelu_kernel(tc, xT, w, wgt, b, wgo, offs, offs2, out):
         scratch = keep.tile([P, 2], F32, name="scratch")
         wgt_t = [keep.tile([P, J], F32, name=f"wgt{h}", align_bytes=64) for h in range(HALVES)]
         wgt_late = keep.tile([P, J], F32, name="wgt_late")
-        wgo_t = keep.tile([P, S], F32, name="wgo_t")
+        wgo_t = [keep.tile([P, J], F32, name=f"wgo{h}") for h in range(HALVES)]
         x = [[keep.tile([P, T], F32, name=f"x{a}_{i}") for i in range(PACK)] for a in range(PASSES)]
         w_raw = [[keep.tile([P, PACK, W_COLS], F32, name=f"wraw{a}_{c}") for c in range(HALVES)] for a in range(PASSES)]
         window = [keep.tile([P, T], F32, name=f"window{m}") for m in range(M_TILES)]
         picked = [[keep.tile([P, PACK, J], F32, name=f"picked{a}_{h}") for h in range(HALVES)] for a in range(PASSES)]
         x_bf = [keep.tile([P, S, PACK], BF16, name=f"xbf{a}", align_bytes=64) for a in range(PASSES)]
         w_bf = [[keep.tile([P, W_COLS, PACK], BF16, name=f"wbf{a}_{c}", align_bytes=64) for c in range(HALVES)] for a in range(PASSES)]
-        x_codes = [keep.tile([P, S], U32, name=f"xc{a}", tag=("xc0", "wgt0", "xc2")[a], align_bytes=64) for a in range(PASSES)]
+        x_codes = [keep.tile([P, S], U32, name=f"xc{a}", tag=("wgt1", "wgt0", "xc2")[a], align_bytes=64) for a in range(PASSES)]
         x_scales = [keep.tile([P, S], U8, name=f"xs{a}", align_bytes=64) for a in range(PASSES)]
         w_codes = [[keep.tile([P, W_COLS], U32, name=f"wc{a}_{c}", align_bytes=64) for c in range(HALVES)] for a in range(PASSES)]
         w_scales = [[keep.tile([P, W_COLS], U8, name=f"ws{a}_{c}", align_bytes=64) for c in range(HALVES)] for a in range(PASSES)]
@@ -72,27 +72,28 @@ def tile_list_hboth_gelu_kernel(tc, xT, w, wgt, b, wgo, offs, offs2, out):
         nc.scalar.dma_start(out=wgt_t[0][:], in_=wgt[:, 0:J])
         load_x(0, 0)
         nc.sync.dma_start(out=wgt_t[1][:], in_=wgt[:, J:S])
+        nc.sync.dma_start(lists_out[:], offs2)
+        nc.sync.dma_start(out=bias_rows[0:M_TILES, :], in_=b.rearrange("(m p) -> m p", p=P))
         load_x(0, 1)
         load_x(0, 2)
         load_x(0, 3)
         load_x(1, 0)
         load_x(1, 1)
         load_x(1, 2)
-        load_w(0, 0)
         load_x(1, 3)
         load_x(2, 0)
         load_x(2, 1)
         load_x(2, 2)
         load_x(2, 3)
-        nc.sync.dma_start(out=wgt_late[:], in_=wgt[:, J:S])
+        load_w(0, 0)
         load_w(1, 0)
         load_w(2, 0)
-        nc.sync.dma_start(lists_out[:], offs2)
-        nc.sync.dma_start(out=bias_rows[0:M_TILES, :], in_=b.rearrange("(m p) -> m p", p=P))
-        nc.sync.dma_start(out=wgo_t[:], in_=wgo)
         load_w(0, 1)
+        nc.sync.dma_start(out=wgo_t[0][:], in_=wgo[:, 0:J])
+        nc.sync.dma_start(out=wgt_late[:], in_=wgt[:, J:S])
         load_w(1, 1)
         load_w(2, 1)
+        nc.sync.dma_start(out=wgo_t[1][:], in_=wgo[:, J:S])
 
         nc.vector.memset(window[0][:], 0.0)
         nc.vector.memset(window[1][:], 0.0)
@@ -106,7 +107,7 @@ def tile_list_hboth_gelu_kernel(tc, xT, w, wgt, b, wgo, offs, offs2, out):
             nc.vector.tensor_tensor(
                 picked[a][h][:, i, :],
                 x[a][i][:].indirect(lists_in[:, h * LIST_HALF : (h + 1) * LIST_HALF]),
-                (wgt_late if (a, h) == (2, 1) and i >= 1 else wgt_t[h])[:],
+                (wgt_late if (a, h) == (2, 1) and i < 2 else wgt_t[h])[:],
                 MULT,
             )
 
@@ -162,7 +163,7 @@ def tile_list_hboth_gelu_kernel(tc, xT, w, wgt, b, wgo, offs, offs2, out):
             nc.vector.tensor_tensor(
                 window[m][:].indirect(lists_out[:, h * LIST_HALF : (h + 1) * LIST_HALF]),
                 y[m][:, h * J : (h + 1) * J],
-                wgo_t[:, h * J : (h + 1) * J],
+                wgo_t[h][:],
                 MULT,
             )
 
@@ -176,11 +177,10 @@ def tile_list_hboth_gelu_kernel(tc, xT, w, wgt, b, wgo, offs, offs2, out):
         gather(0, 0, 2)
         gather(0, 1, 2)
         gather(0, 0, 3)
-        round_x(0, 0)
-        quantize_x(0, 0)
         gather(0, 1, 3)
+        round_x(0, 0)
         round_x(0, 1)
-        quantize_x(0, 1)
+        quantize_x_pass(0)
         gather(1, 0, 0)
         gather(1, 1, 0)
         gather(1, 0, 1)
@@ -188,42 +188,40 @@ def tile_list_hboth_gelu_kernel(tc, xT, w, wgt, b, wgo, offs, offs2, out):
         gather(1, 0, 2)
         gather(1, 1, 2)
         gather(1, 0, 3)
-        round_x(1, 0)
         gather(1, 1, 3)
+        round_x(1, 0)
         round_x(1, 1)
         quantize_x_pass(1)
-        round_w(nc.scalar.copy, 0, 0, 0, P)
-        round_w(nc.scalar.copy, 0, 0, P, W_COLS)
-        quantize_w(0, 0)
         gather(2, 0, 0)
         gather(2, 1, 0)
-        round_w(nc.scalar.copy, 1, 0, 0, P)
-        round_w(nc.scalar.copy, 1, 0, P, W_COLS)
-        quantize_w(1, 0)
         gather(2, 0, 1)
         gather(2, 1, 1)
         gather(2, 0, 2)
+        gather(2, 1, 2)
         gather(2, 0, 3)
+        gather(2, 1, 3)
         round_x(2, 0)
         quantize_x(2, 0)
-        gather(2, 1, 2)
-        gather(2, 1, 3)
         round_x(2, 1)
         quantize_x(2, 1)
-        round_w(nc.vector.tensor_copy, 2, 0, 0, W_COLS)
+        round_w(nc.vector.tensor_copy, 0, 0, 0, W_COLS)
+        quantize_w(0, 0)
+        round_w(nc.scalar.copy, 1, 0, 0, W_COLS)
+        quantize_w(1, 0)
+        round_w(nc.scalar.copy, 2, 0, 0, P)
+        round_w(nc.vector.tensor_copy, 2, 0, P, W_COLS)
         quantize_w(2, 0)
         multiply(acc_half[0][0], 0, 0, J)
         multiply(acc_half[1][0], 1, 0, J)
-        round_w(nc.scalar.copy, 0, 1, 0, P)
-        round_w(nc.scalar.copy, 0, 1, P, W_COLS)
+        round_w(nc.scalar.copy, 0, 1, 0, W_COLS)
         quantize_w(0, 1)
         scatter(0, 0)
+        scatter(1, 0)
+        multiply(acc_half[0][1], 0, J, S)
         round_w(nc.scalar.copy, 1, 1, 0, W_COLS)
         quantize_w(1, 1)
-        scatter(1, 0)
         round_w(nc.scalar.copy, 2, 1, 0, W_COLS)
         quantize_w(2, 1)
-        multiply(acc_half[0][1], 0, J, S)
         multiply(acc_half[1][1], 1, J, S)
         scatter(0, 1)
         store(0)

@@ -20,11 +20,12 @@ PACK = 4
 K_PASS = P * PACK
 PASSES = K // K_PASS
 HALVES = 2
-J = S // HALVES
-W_COLS = M // HALVES
+ENTRIES = S // HALVES
+LIST_COLS = ENTRIES // 16
 M_TILES = M // P
-LIST = S // 16
-LIST_HALF = LIST // HALVES
+W_COLS = M // HALVES
+COPY_RUN = 4
+ALIGN = 64
 
 
 def tile_list_hboth_gelu_kernel(tc, xT, w, wgt, b, wgo, offs, offs2, out):
@@ -33,28 +34,66 @@ def tile_list_hboth_gelu_kernel(tc, xT, w, wgt, b, wgo, offs, offs2, out):
         keep = ctx.enter_context(tc.tile_pool(name="keep", bufs=1))
         psum = ctx.enter_context(tc.psum_pool(name="psum", bufs=1))
 
-        lists_in = keep.tile([P, LIST], U16, name="lists_in")
-        lists_out = keep.tile([P, LIST], U16, name="lists_out")
+        lists_in = keep.tile([P, S // 16], U16, name="lists_in")
+        lists_out = keep.tile([P, S // 16], U16, name="lists_out")
         bias_rows = keep.tile([P, P], F32, name="bias_rows")
         ident = keep.tile([P, P], F32, name="ident")
         bias = keep.tile([P, M_TILES], F32, name="bias")
         scratch = keep.tile([P, 2], F32, name="scratch")
-        wgt_t = [keep.tile([P, J], F32, name=f"wgt{h}", align_bytes=64) for h in range(HALVES)]
-        wgt_late = keep.tile([P, J], F32, name="wgt_late")
-        wgo_t = [keep.tile([P, J], F32, name=f"wgo{h}") for h in range(HALVES)]
+        wgt_half = [
+            keep.tile([P, ENTRIES], F32, name=f"wgt_half{h}", tag=f"wgt_half{h}", align_bytes=ALIGN)
+            for h in range(HALVES)
+        ]
+        wgt_late = keep.tile([P, ENTRIES], F32, name="wgt_late", tag="wgt_late", align_bytes=ALIGN)
+        wgo_half = [keep.tile([P, ENTRIES], F32, name=f"wgo_half{h}") for h in range(HALVES)]
         x = [[keep.tile([P, T], F32, name=f"x{a}_{i}") for i in range(PACK)] for a in range(PASSES)]
-        w_raw = [[keep.tile([P, PACK, W_COLS], F32, name=f"wraw{a}_{c}") for c in range(HALVES)] for a in range(PASSES)]
+        w_raw = [
+            [keep.tile([P, PACK, W_COLS], F32, name=f"w_raw{a}_{c}") for c in range(HALVES)] for a in range(PASSES)
+        ]
         window = [keep.tile([P, T], F32, name=f"window{m}") for m in range(M_TILES)]
-        picked = [[keep.tile([P, PACK, J], F32, name=f"picked{a}_{h}") for h in range(HALVES)] for a in range(PASSES)]
-        x_bf = [keep.tile([P, S, PACK], BF16, name=f"xbf{a}", align_bytes=64) for a in range(PASSES)]
-        w_bf = [[keep.tile([P, W_COLS, PACK], BF16, name=f"wbf{a}_{c}", align_bytes=64) for c in range(HALVES)] for a in range(PASSES)]
-        x_codes = [keep.tile([P, S], U32, name=f"xc{a}", tag=("wgt1", "wgt0", "xc2")[a], align_bytes=64) for a in range(PASSES)]
-        x_scales = [keep.tile([P, S], U8, name=f"xs{a}", align_bytes=64) for a in range(PASSES)]
-        w_codes = [[keep.tile([P, W_COLS], U32, name=f"wc{a}_{c}", align_bytes=64) for c in range(HALVES)] for a in range(PASSES)]
-        w_scales = [[keep.tile([P, W_COLS], U8, name=f"ws{a}_{c}", align_bytes=64) for c in range(HALVES)] for a in range(PASSES)]
+        picked = [
+            [keep.tile([P, PACK, ENTRIES], F32, name=f"picked{a}_{h}") for h in range(HALVES)] for a in range(PASSES)
+        ]
+        x_bf = [keep.tile([P, S, PACK], BF16, name=f"x_bf{a}", align_bytes=ALIGN) for a in range(PASSES)]
+        w_bf = [
+            [keep.tile([P, W_COLS, PACK], BF16, name=f"w_bf{a}_{c}", align_bytes=ALIGN) for c in range(HALVES)]
+            for a in range(PASSES)
+        ]
+        second_codes = keep.tile(
+            [P, (PASSES - 1) * ENTRIES], U32, name="second_codes", tag="wgt_late", align_bytes=ALIGN
+        )
+        x_codes = [
+            [
+                keep.tile([P, ENTRIES], U32, name="x_codes0_0", tag="wgt_half1", align_bytes=ALIGN)[:],
+                second_codes[:, 0:ENTRIES],
+            ],
+            [
+                keep.tile([P, ENTRIES], U32, name="x_codes1_0", tag="wgt_half0", align_bytes=ALIGN)[:],
+                second_codes[:, ENTRIES : 2 * ENTRIES],
+            ],
+            [keep.tile([P, ENTRIES], U32, name=f"x_codes2_{h}", align_bytes=ALIGN)[:] for h in range(HALVES)],
+        ]
+        x_scales = [keep.tile([P, S], U8, name=f"x_scales{a}", align_bytes=ALIGN) for a in range(PASSES)]
+        w_codes = [
+            [keep.tile([P, W_COLS], U32, name=f"w_codes{a}_{c}", align_bytes=ALIGN) for c in range(HALVES)]
+            for a in range(PASSES)
+        ]
+        w_scales = [
+            [keep.tile([P, W_COLS], U8, name=f"w_scales{a}_{c}", align_bytes=ALIGN) for c in range(HALVES)]
+            for a in range(PASSES)
+        ]
         y = [keep.tile([P, S], F32, name=f"y{m}") for m in range(M_TILES)]
-        bias_bank = psum.tile([P, P], F32, name="bias_bank", tag="acc3_1")
-        acc_half = [[psum.tile([P, J], F32, name=f"acc{m}_{h}", tag=f"acc{m}_{h}") for h in range(HALVES)] for m in range(M_TILES)]
+        bias_bank = psum.tile([P, P], F32, name="bias_bank", tag=f"acc{M_TILES - 1}_{HALVES - 1}")
+        acc = [
+            [psum.tile([P, ENTRIES], F32, name=f"acc{m}_{h}", tag=f"acc{m}_{h}") for h in range(HALVES)]
+            for m in range(M_TILES)
+        ]
+
+        def half(h):
+            return slice(h * ENTRIES, (h + 1) * ENTRIES)
+
+        def half_list(h):
+            return slice(h * LIST_COLS, (h + 1) * LIST_COLS)
 
         def load_x(a, i):
             planes = xT[a * K_PASS : (a + 1) * K_PASS, :].rearrange("(p i) t -> p i t", i=PACK)
@@ -64,176 +103,138 @@ def tile_list_hboth_gelu_kernel(tc, xT, w, wgt, b, wgo, offs, offs2, out):
             rows = w[a * K_PASS : (a + 1) * K_PASS, c * W_COLS : (c + 1) * W_COLS]
             nc.sync.dma_start(out=w_raw[a][c][:], in_=rows.rearrange("(p i) n -> p i n", i=PACK))
 
-        nc.gpsimd.memset(scratch[:], 0.0)
-        nc.gpsimd.memset(bias_rows[:], 0.0)
-        nc.scalar.activation(scratch[:, 1:2], scratch[:, 0:1], GELU)
-
-        nc.sync.dma_start(lists_in[:], offs)
-        nc.scalar.dma_start(out=wgt_t[0][:], in_=wgt[:, 0:J])
-        load_x(0, 0)
-        nc.sync.dma_start(out=wgt_t[1][:], in_=wgt[:, J:S])
-        nc.sync.dma_start(lists_out[:], offs2)
-        nc.sync.dma_start(out=bias_rows[0:M_TILES, :], in_=b.rearrange("(m p) -> m p", p=P))
-        load_x(0, 1)
-        load_x(0, 2)
-        load_x(0, 3)
-        load_x(1, 0)
-        load_x(1, 1)
-        load_x(1, 2)
-        load_x(1, 3)
-        load_x(2, 0)
-        load_x(2, 1)
-        load_x(2, 2)
-        load_x(2, 3)
-        load_w(0, 0)
-        load_w(1, 0)
-        load_w(2, 0)
-        load_w(0, 1)
-        nc.sync.dma_start(out=wgo_t[0][:], in_=wgo[:, 0:J])
-        nc.sync.dma_start(out=wgt_late[:], in_=wgt[:, J:S])
-        load_w(1, 1)
-        load_w(2, 1)
-        nc.sync.dma_start(out=wgo_t[1][:], in_=wgo[:, J:S])
-
-        nc.vector.memset(window[0][:], 0.0)
-        nc.vector.memset(window[1][:], 0.0)
-        make_identity(nc, ident[:])
-        nc.gpsimd.memset(window[2][:], 0.0)
-        nc.gpsimd.memset(window[3][:], 0.0)
-        nc.tensor.transpose(bias_bank[:], bias_rows[:], ident[:])
-        nc.scalar.copy(out=bias[:], in_=bias_bank[:, 0:M_TILES])
-
-        def gather(a, h, i):
+        def gather(a, i, h):
+            late = a == PASSES - 1 and h == 1 and i < 2
             nc.vector.tensor_tensor(
                 picked[a][h][:, i, :],
-                x[a][i][:].indirect(lists_in[:, h * LIST_HALF : (h + 1) * LIST_HALF]),
-                (wgt_late if (a, h) == (2, 1) and i < 2 else wgt_t[h])[:],
+                x[a][i][:].indirect(lists_in[:, half_list(h)]),
+                (wgt_late if late else wgt_half[h])[:],
                 MULT,
             )
 
         def interleave(copy, grouped, planes):
             copy(
-                out=grouped.rearrange("p (c q) i -> p c i q", q=4),
-                in_=planes.rearrange("p i (c q) -> p c i q", q=4),
+                out=grouped.rearrange("p (c r) i -> p c i r", r=COPY_RUN),
+                in_=planes.rearrange("p i (c r) -> p c i r", r=COPY_RUN),
             )
 
-        def round_x(a, h):
-            interleave(nc.scalar.copy, x_bf[a][:, h * J : (h + 1) * J, :], picked[a][h][:])
+        def round_x(a, h, scalar_cols):
+            grouped = x_bf[a][:, half(h), :]
+            interleave(nc.scalar.copy, grouped[:, 0:scalar_cols, :], picked[a][h][:, :, 0:scalar_cols])
+            if scalar_cols < ENTRIES:
+                rest = slice(scalar_cols, ENTRIES)
+                interleave(nc.vector.tensor_copy, grouped[:, rest, :], picked[a][h][:, :, rest])
 
         def quantize_x(a, h):
-            js = slice(h * J, (h + 1) * J)
             nc.vector.quantize_mx(
-                out=x_codes[a][:, js].bitcast(FP8X4),
-                scales=x_scales[a][:, js],
-                in_=x_bf[a][:, js, :].rearrange("p j i -> p (j i)"),
+                out=x_codes[a][h].bitcast(FP8X4),
+                scales=x_scales[a][:, half(h)],
+                in_=x_bf[a][:, half(h), :].rearrange("p j i -> p (j i)"),
             )
 
-        def quantize_x_pass(a):
-            nc.vector.quantize_mx(
-                out=x_codes[a][:].bitcast(FP8X4),
-                scales=x_scales[a][:],
-                in_=x_bf[a][:].rearrange("p j i -> p (j i)"),
-            )
-
-        def round_w(copy, a, c, n0, n1):
-            interleave(copy, w_bf[a][c][:, n0:n1, :], w_raw[a][c][:, :, n0:n1])
-
-        def quantize_w(a, c):
+        def prepare_w(a, c, scalar_cols):
+            if scalar_cols > 0:
+                interleave(nc.scalar.copy, w_bf[a][c][:, 0:scalar_cols, :], w_raw[a][c][:, :, 0:scalar_cols])
+            if scalar_cols < W_COLS:
+                rest = slice(scalar_cols, W_COLS)
+                interleave(nc.vector.tensor_copy, w_bf[a][c][:, rest, :], w_raw[a][c][:, :, rest])
             nc.vector.quantize_mx(
                 out=w_codes[a][c][:].bitcast(FP8X4),
                 scales=w_scales[a][c][:],
                 in_=w_bf[a][c][:].rearrange("p n i -> p (n i)"),
             )
 
-        def multiply(bank, m, j0, j1):
-            c, n0 = m // 2, m % 2 * P
+        def project(m, h):
+            c, n0 = m * P // W_COLS, m * P % W_COLS
             for a in range(PASSES):
                 nc.tensor.matmul_mx(
-                    out=bank[:],
+                    out=acc[m][h][:],
                     lhsT=w_codes[a][c][:, n0 : n0 + P].bitcast(FP8X4),
                     lhsT_scale=w_scales[a][c][:, n0 : n0 + P],
-                    rhs=x_codes[a][:, j0:j1].bitcast(FP8X4),
-                    rhs_scale=x_scales[a][:, j0:j1],
+                    rhs=x_codes[a][h].bitcast(FP8X4),
+                    rhs_scale=x_scales[a][:, half(h)],
                     start=(a == 0),
                     stop=(a == PASSES - 1),
                 )
-            nc.scalar.activation(y[m][:, j0:j1], bank[:], GELU, bias=bias[:, m : m + 1])
+            nc.scalar.activation(y[m][:, half(h)], acc[m][h][:], GELU, bias=bias[:, m : m + 1])
 
         def scatter(m, h):
             nc.vector.tensor_tensor(
-                window[m][:].indirect(lists_out[:, h * LIST_HALF : (h + 1) * LIST_HALF]),
-                y[m][:, h * J : (h + 1) * J],
-                wgo_t[h][:],
+                window[m][:].indirect(lists_out[:, half_list(h)]),
+                y[m][:, half(h)],
+                wgo_half[h][:],
                 MULT,
             )
 
         def store(m):
             nc.sync.dma_start(out=out[m * P : (m + 1) * P, :], in_=window[m][:])
 
-        gather(0, 0, 0)
-        gather(0, 1, 0)
-        gather(0, 0, 1)
-        gather(0, 1, 1)
-        gather(0, 0, 2)
-        gather(0, 1, 2)
-        gather(0, 0, 3)
-        gather(0, 1, 3)
-        round_x(0, 0)
-        round_x(0, 1)
-        quantize_x_pass(0)
-        gather(1, 0, 0)
-        gather(1, 1, 0)
-        gather(1, 0, 1)
-        gather(1, 1, 1)
-        gather(1, 0, 2)
-        gather(1, 1, 2)
-        gather(1, 0, 3)
-        gather(1, 1, 3)
-        round_x(1, 0)
-        round_x(1, 1)
-        quantize_x_pass(1)
-        gather(2, 0, 0)
-        gather(2, 1, 0)
-        gather(2, 0, 1)
-        gather(2, 1, 1)
-        gather(2, 0, 2)
-        gather(2, 1, 2)
-        gather(2, 0, 3)
-        gather(2, 1, 3)
-        round_x(2, 0)
-        quantize_x(2, 0)
-        round_x(2, 1)
-        quantize_x(2, 1)
-        round_w(nc.vector.tensor_copy, 0, 0, 0, W_COLS)
-        quantize_w(0, 0)
-        round_w(nc.scalar.copy, 1, 0, 0, W_COLS)
-        quantize_w(1, 0)
-        round_w(nc.scalar.copy, 2, 0, 0, P)
-        round_w(nc.vector.tensor_copy, 2, 0, P, W_COLS)
-        quantize_w(2, 0)
-        multiply(acc_half[0][0], 0, 0, J)
-        multiply(acc_half[1][0], 1, 0, J)
-        round_w(nc.scalar.copy, 0, 1, 0, W_COLS)
-        quantize_w(0, 1)
+        nc.gpsimd.memset(scratch[:], 0.0)
+        nc.gpsimd.memset(bias_rows[:], 0.0)
+        nc.scalar.activation(scratch[:, 1:2], scratch[:, 0:1], GELU)
+
+        nc.sync.dma_start(lists_in[:], offs)
+        nc.scalar.dma_start(out=wgt_half[0][:], in_=wgt[:, half(0)])
+        load_x(0, 0)
+        nc.sync.dma_start(out=wgt_half[1][:], in_=wgt[:, half(1)])
+        nc.sync.dma_start(lists_out[:], offs2)
+        nc.sync.dma_start(out=bias_rows[0:M_TILES, :], in_=b.rearrange("(m p) -> m p", p=P))
+        for a in range(PASSES):
+            for i in range(PACK):
+                if (a, i) != (0, 0):
+                    load_x(a, i)
+        for a in range(PASSES):
+            load_w(a, 0)
+        load_w(0, 1)
+        nc.sync.dma_start(out=wgo_half[0][:], in_=wgo[:, half(0)])
+        nc.sync.dma_start(out=wgt_late[:], in_=wgt[:, half(1)])
+        for a in range(1, PASSES):
+            load_w(a, 1)
+        nc.sync.dma_start(out=wgo_half[1][:], in_=wgo[:, half(1)])
+
+        nc.vector.memset(window[0][:], 0.0)
+        nc.vector.memset(window[1][:], 0.0)
+        make_identity(nc, ident[:])
+        nc.gpsimd.memset(window[2][:], 0.0)
+        nc.gpsimd.memset(window[3][:], 0.0)
+
+        nc.tensor.transpose(bias_bank[:], bias_rows[:], ident[:])
+        nc.scalar.copy(out=bias[:], in_=bias_bank[:, 0:M_TILES])
+
+        for a in range(PASSES):
+            for i in range(PACK):
+                for h in range(HALVES):
+                    gather(a, i, h)
+            if a < PASSES - 1:
+                for h in range(HALVES):
+                    round_x(a, h, ENTRIES)
+                for h in range(HALVES):
+                    quantize_x(a, h)
+            else:
+                for h in range(HALVES):
+                    round_x(a, h, ENTRIES // 2)
+                    quantize_x(a, h)
+
+        prepare_w(0, 0, 0)
+        prepare_w(1, 0, W_COLS)
+        prepare_w(2, 0, W_COLS // 2)
+
+        project(0, 0)
+        project(1, 0)
+        prepare_w(0, 1, W_COLS)
         scatter(0, 0)
         scatter(1, 0)
-        multiply(acc_half[0][1], 0, J, S)
-        round_w(nc.scalar.copy, 1, 1, 0, W_COLS)
-        quantize_w(1, 1)
-        round_w(nc.scalar.copy, 2, 1, 0, W_COLS)
-        quantize_w(2, 1)
-        multiply(acc_half[1][1], 1, J, S)
-        scatter(0, 1)
-        store(0)
-        scatter(1, 1)
-        store(1)
-        multiply(acc_half[2][0], 2, 0, J)
-        multiply(acc_half[3][0], 3, 0, J)
-        scatter(2, 0)
-        scatter(3, 0)
-        multiply(acc_half[2][1], 2, J, S)
-        multiply(acc_half[3][1], 3, J, S)
-        scatter(2, 1)
-        store(2)
-        scatter(3, 1)
-        store(3)
+        project(0, 1)
+        prepare_w(1, 1, W_COLS)
+        prepare_w(2, 1, W_COLS)
+        project(1, 1)
+        for m in (0, 1):
+            scatter(m, 1)
+            store(m)
+        for h in range(HALVES):
+            for m in (2, 3):
+                project(m, h)
+            for m in (2, 3):
+                scatter(m, h)
+                if h == HALVES - 1:
+                    store(m)

from contextlib import ExitStack

import concourse.mybir as mybir
from concourse.masks import make_identity

K, M, T, S = 1536, 512, 1024, 512
FLOPS = 2 * K * M * S

F32 = mybir.dt.float32
BF16 = mybir.dt.bfloat16
U32 = mybir.dt.uint32
U16 = mybir.dt.uint16
U8 = mybir.dt.uint8
FP8X4 = mybir.dt.float8_e4m3fn_x4
MULT = mybir.AluOpType.mult
GELU = mybir.ActivationFunctionType.Gelu_apprx_tanh

P = 128
PACK = 4
K_PASS = P * PACK
PASSES = K // K_PASS
HALVES = 2
ENTRIES = S // HALVES
LIST_COLS = ENTRIES // 16
M_TILES = M // P
W_COLS = M // HALVES
COPY_RUN = 4
ALIGN = 64


def tile_list_hboth_gelu_kernel(tc, xT, w, wgt, b, wgo, offs, offs2, out):
    nc = tc.nc
    with ExitStack() as ctx:
        keep = ctx.enter_context(tc.tile_pool(name="keep", bufs=1))
        psum = ctx.enter_context(tc.psum_pool(name="psum", bufs=1))

        lists_in = keep.tile([P, S // 16], U16, name="lists_in")
        lists_out = keep.tile([P, S // 16], U16, name="lists_out")
        bias_rows = keep.tile([P, P], F32, name="bias_rows")
        ident = keep.tile([P, P], F32, name="ident")
        bias = keep.tile([P, M_TILES], F32, name="bias")
        scratch = keep.tile([P, 2], F32, name="scratch")
        wgt_half = [
            keep.tile([P, ENTRIES], F32, name=f"wgt_half{h}", tag=f"wgt_half{h}", align_bytes=ALIGN)
            for h in range(HALVES)
        ]
        wgt_late = keep.tile([P, ENTRIES], F32, name="wgt_late", tag="wgt_late", align_bytes=ALIGN)
        wgo_half = [keep.tile([P, ENTRIES], F32, name=f"wgo_half{h}") for h in range(HALVES)]
        x = [[keep.tile([P, T], F32, name=f"x{a}_{i}") for i in range(PACK)] for a in range(PASSES)]
        w_raw = [
            [keep.tile([P, PACK, W_COLS], F32, name=f"w_raw{a}_{c}") for c in range(HALVES)] for a in range(PASSES)
        ]
        window = [keep.tile([P, T], F32, name=f"window{m}") for m in range(M_TILES)]
        picked = [
            [keep.tile([P, PACK, ENTRIES], F32, name=f"picked{a}_{h}") for h in range(HALVES)] for a in range(PASSES)
        ]
        x_bf = [keep.tile([P, S, PACK], BF16, name=f"x_bf{a}", align_bytes=ALIGN) for a in range(PASSES)]
        w_bf = [
            [keep.tile([P, W_COLS, PACK], BF16, name=f"w_bf{a}_{c}", align_bytes=ALIGN) for c in range(HALVES)]
            for a in range(PASSES)
        ]
        second_codes = keep.tile(
            [P, (PASSES - 1) * ENTRIES], U32, name="second_codes", tag="wgt_late", align_bytes=ALIGN
        )
        x_codes = [
            [
                keep.tile([P, ENTRIES], U32, name="x_codes0_0", tag="wgt_half1", align_bytes=ALIGN)[:],
                second_codes[:, 0:ENTRIES],
            ],
            [
                keep.tile([P, ENTRIES], U32, name="x_codes1_0", tag="wgt_half0", align_bytes=ALIGN)[:],
                second_codes[:, ENTRIES : 2 * ENTRIES],
            ],
            [keep.tile([P, ENTRIES], U32, name=f"x_codes2_{h}", align_bytes=ALIGN)[:] for h in range(HALVES)],
        ]
        x_scales = [keep.tile([P, S], U8, name=f"x_scales{a}", align_bytes=ALIGN) for a in range(PASSES)]
        w_codes = [
            [keep.tile([P, W_COLS], U32, name=f"w_codes{a}_{c}", align_bytes=ALIGN) for c in range(HALVES)]
            for a in range(PASSES)
        ]
        w_scales = [
            [keep.tile([P, W_COLS], U8, name=f"w_scales{a}_{c}", align_bytes=ALIGN) for c in range(HALVES)]
            for a in range(PASSES)
        ]
        y = [keep.tile([P, S], F32, name=f"y{m}") for m in range(M_TILES)]
        bias_bank = psum.tile([P, P], F32, name="bias_bank", tag=f"acc{M_TILES - 1}_{HALVES - 1}")
        acc = [
            [psum.tile([P, ENTRIES], F32, name=f"acc{m}_{h}", tag=f"acc{m}_{h}") for h in range(HALVES)]
            for m in range(M_TILES)
        ]

        def half(h):
            return slice(h * ENTRIES, (h + 1) * ENTRIES)

        def half_list(h):
            return slice(h * LIST_COLS, (h + 1) * LIST_COLS)

        def load_x(a, i):
            planes = xT[a * K_PASS : (a + 1) * K_PASS, :].rearrange("(p i) t -> p i t", i=PACK)
            nc.sync.dma_start(out=x[a][i][:], in_=planes[:, i, :])

        def load_w(a, c):
            rows = w[a * K_PASS : (a + 1) * K_PASS, c * W_COLS : (c + 1) * W_COLS]
            nc.sync.dma_start(out=w_raw[a][c][:], in_=rows.rearrange("(p i) n -> p i n", i=PACK))

        def gather(a, i, h):
            late = a == PASSES - 1 and h == 1 and i < 2
            nc.vector.tensor_tensor(
                picked[a][h][:, i, :],
                x[a][i][:].indirect(lists_in[:, half_list(h)]),
                (wgt_late if late else wgt_half[h])[:],
                MULT,
            )

        def interleave(copy, grouped, planes):
            copy(
                out=grouped.rearrange("p (c r) i -> p c i r", r=COPY_RUN),
                in_=planes.rearrange("p i (c r) -> p c i r", r=COPY_RUN),
            )

        def round_x(a, h, scalar_cols):
            grouped = x_bf[a][:, half(h), :]
            interleave(nc.scalar.copy, grouped[:, 0:scalar_cols, :], picked[a][h][:, :, 0:scalar_cols])
            if scalar_cols < ENTRIES:
                rest = slice(scalar_cols, ENTRIES)
                interleave(nc.vector.tensor_copy, grouped[:, rest, :], picked[a][h][:, :, rest])

        def quantize_x(a, h):
            nc.vector.quantize_mx(
                out=x_codes[a][h].bitcast(FP8X4),
                scales=x_scales[a][:, half(h)],
                in_=x_bf[a][:, half(h), :].rearrange("p j i -> p (j i)"),
            )

        def prepare_w(a, c, scalar_cols):
            if scalar_cols > 0:
                interleave(nc.scalar.copy, w_bf[a][c][:, 0:scalar_cols, :], w_raw[a][c][:, :, 0:scalar_cols])
            if scalar_cols < W_COLS:
                rest = slice(scalar_cols, W_COLS)
                interleave(nc.vector.tensor_copy, w_bf[a][c][:, rest, :], w_raw[a][c][:, :, rest])
            nc.vector.quantize_mx(
                out=w_codes[a][c][:].bitcast(FP8X4),
                scales=w_scales[a][c][:],
                in_=w_bf[a][c][:].rearrange("p n i -> p (n i)"),
            )

        def project(m, h):
            c, n0 = m * P // W_COLS, m * P % W_COLS
            for a in range(PASSES):
                nc.tensor.matmul_mx(
                    out=acc[m][h][:],
                    lhsT=w_codes[a][c][:, n0 : n0 + P].bitcast(FP8X4),
                    lhsT_scale=w_scales[a][c][:, n0 : n0 + P],
                    rhs=x_codes[a][h].bitcast(FP8X4),
                    rhs_scale=x_scales[a][:, half(h)],
                    start=(a == 0),
                    stop=(a == PASSES - 1),
                )
            nc.scalar.activation(y[m][:, half(h)], acc[m][h][:], GELU, bias=bias[:, m : m + 1])

        def scatter(m, h):
            nc.vector.tensor_tensor(
                window[m][:].indirect(lists_out[:, half_list(h)]),
                y[m][:, half(h)],
                wgo_half[h][:],
                MULT,
            )

        def store(m):
            nc.sync.dma_start(out=out[m * P : (m + 1) * P, :], in_=window[m][:])

        nc.gpsimd.memset(scratch[:], 0.0)
        nc.gpsimd.memset(bias_rows[:], 0.0)
        nc.scalar.activation(scratch[:, 1:2], scratch[:, 0:1], GELU)

        nc.sync.dma_start(lists_in[:], offs)
        nc.scalar.dma_start(out=wgt_half[0][:], in_=wgt[:, half(0)])
        load_x(0, 0)
        nc.sync.dma_start(out=wgt_half[1][:], in_=wgt[:, half(1)])
        nc.sync.dma_start(lists_out[:], offs2)
        nc.sync.dma_start(out=bias_rows[0:M_TILES, :], in_=b.rearrange("(m p) -> m p", p=P))
        for a in range(PASSES):
            for i in range(PACK):
                if (a, i) != (0, 0):
                    load_x(a, i)
        for a in range(PASSES):
            load_w(a, 0)
        load_w(0, 1)
        nc.sync.dma_start(out=wgo_half[0][:], in_=wgo[:, half(0)])
        nc.sync.dma_start(out=wgt_late[:], in_=wgt[:, half(1)])
        for a in range(1, PASSES):
            load_w(a, 1)
        nc.sync.dma_start(out=wgo_half[1][:], in_=wgo[:, half(1)])

        nc.vector.memset(window[0][:], 0.0)
        nc.vector.memset(window[1][:], 0.0)
        make_identity(nc, ident[:])
        nc.gpsimd.memset(window[2][:], 0.0)
        nc.gpsimd.memset(window[3][:], 0.0)

        nc.tensor.transpose(bias_bank[:], bias_rows[:], ident[:])
        nc.scalar.copy(out=bias[:], in_=bias_bank[:, 0:M_TILES])

        for a in range(PASSES):
            for i in range(PACK):
                for h in range(HALVES):
                    gather(a, i, h)
            if a < PASSES - 1:
                for h in range(HALVES):
                    round_x(a, h, ENTRIES)
                for h in range(HALVES):
                    quantize_x(a, h)
            else:
                for h in range(HALVES):
                    round_x(a, h, ENTRIES // 2)
                    quantize_x(a, h)

        prepare_w(0, 0, 0)
        prepare_w(1, 0, W_COLS)
        prepare_w(2, 0, W_COLS // 2)

        project(0, 0)
        project(1, 0)
        prepare_w(0, 1, W_COLS)
        scatter(0, 0)
        scatter(1, 0)
        project(0, 1)
        prepare_w(1, 1, W_COLS)
        prepare_w(2, 1, W_COLS)
        project(1, 1)
        for m in (0, 1):
            scatter(m, 1)
            store(m)
        for h in range(HALVES):
            for m in (2, 3):
                project(m, h)
            for m in (2, 3):
                scatter(m, h)
                if h == HALVES - 1:
                    store(m)
